import numpy as np
import ml_dtypes


def mxq(x, axis, fmt="e4m3"):
    dtype, down = {"e4m3": (ml_dtypes.float8_e4m3fn, 7), "e5m2": (ml_dtypes.float8_e5m2, 14)}[fmt]
    v = np.moveaxis(np.asarray(x, np.float32).astype(ml_dtypes.bfloat16).astype(np.float64), axis, -1)
    blocks = v.reshape(v.shape[:-1] + (-1, 32))
    amax = np.abs(blocks).max(-1, keepdims=True)
    byte = np.maximum(np.where(amax > 0, np.frexp(amax)[1] - 1 + 127, 0) - down, 1)
    scale = np.exp2(byte - 127.0)
    codes = (blocks / scale).astype(np.float32).astype(dtype).astype(np.float64)
    return np.moveaxis((codes * scale).reshape(v.shape), -1, axis)


WIDE = False


def mx_kscale(k):
    if not WIDE:
        return np.ones(k)
    levels = np.array([10, -10, 5, -5, 0])
    if k % 512:
        return np.exp2(np.random.permutation(np.resize(levels, k // 32))).repeat(32)
    a = np.empty((k // 512, 16))
    for p in range(k // 512):
        a[p, :8] = np.random.permutation(np.resize(levels, 8))
        for g in range(8):
            far = levels[np.abs(levels - a[p, g]) >= 10]
            a[p, g + 8] = far[np.random.randint(len(far))]
    return np.exp2(a.ravel()).repeat(32)


BF16 = ml_dtypes.bfloat16


def bf(x):
    return np.asarray(x, np.float32).astype(BF16)


def f64(x):
    return np.asarray(x).astype(np.float64)


E2M1 = np.array([0.0, 0.5, 1.0, 1.5, 2.0, 3.0, 4.0, 6.0, -0.0, -0.5, -1.0, -1.5, -2.0, -3.0, -4.0, -6.0])


def pack_weight(w, fmt):
    k, n = w.shape
    w = f64(bf(w)).reshape(k // 32, 32, n)
    amax = np.abs(w).max(1)
    if fmt == "e4m3":
        byte = np.frexp(amax)[1] - 1 + 127 - 7
    else:
        mant, ex = np.frexp(amax / 6.0)
        byte = np.where(mant > 0.5, ex, ex - 1) + 127
    byte = np.clip(np.where(amax > 0, byte, 1), 1, 254)
    scaled = (w * np.exp2(127.0 - byte)[:, None, :]).reshape(k, n).astype(np.float32)
    by_word = np.ascontiguousarray(scaled.reshape(k // 512, 128, 4, n).transpose(0, 1, 3, 2))
    if fmt == "e4m3":
        words = by_word.astype(ml_dtypes.float8_e4m3fn).view(np.uint8)
    else:
        c = by_word.astype(ml_dtypes.float4_e2m1fn).view(np.uint8) & 0xF
        words = c[..., 0::2] | (c[..., 1::2] << 4)
    return np.ascontiguousarray(words), np.ascontiguousarray(byte.astype(np.uint8).reshape(k // 512, 16, n))


def unpack_weight(words, scales, fmt):
    g, p, n, _ = words.shape
    if fmt == "e4m3":
        vals = np.ascontiguousarray(words).view(ml_dtypes.float8_e4m3fn).astype(np.float64)
    else:
        nib = np.empty((g, p, n, 4), np.uint8)
        nib[..., 0::2] = words & 0xF
        nib[..., 1::2] = words >> 4
        vals = E2M1[nib]
    vals = vals * np.repeat(np.exp2(scales.astype(np.float64) - 127.0), 8, axis=1)[..., None]
    return vals.transpose(0, 1, 3, 2).reshape(g * 512, n)
def pack4(w):
    words, scales = pack_weight(w, "e2m1")
    return words.reshape(words.shape[0], 128, -1), scales


def unpack4(words, scales):
    return unpack_weight(words.reshape(words.shape[0], 128, -1, 2), scales, "e2m1")


B, D, M = 1024, 2048, 1024


def setup_inputs():
    s = mx_kscale(D)
    t = mx_kscale(M)
    x0 = bf(np.random.standard_normal((B, D)))
    a = np.linalg.qr(np.random.standard_normal((D, M)))[0]
    x_words, x_scales = pack4(f64(x0).T * s[:, None])
    a_words, a_scales = pack4(a / s[:, None] * t)
    pinv_words, pinv_scales = pack_weight(a.T / t[:, None], "e4m3")
    return {"x_words": x_words, "x_scales": x_scales,
            "a_words": a_words, "a_scales": a_scales,
            "pinv_words": pinv_words, "pinv_scales": pinv_scales,
            "x0": x0,
            "y": bf(np.random.standard_normal((B, M)) * t),
            "mask": bf(np.random.uniform(0.25, 1.0, (B, M)))}


def reference(x_words, x_scales, a_words, a_scales, pinv_words, pinv_scales, x0, y, mask):
    x = unpack4(x_words, x_scales)
    a = unpack4(a_words, a_scales)
    pinv = unpack_weight(pinv_words, pinv_scales, "e4m3")
    measured = x.T @ a
    r = f64(mask) * (f64(y) - measured)
    return f64(x0) + (mxq(r, 1, "e4m3") @ pinv)

@@ -1,0 +1,226 @@
+from contextlib import ExitStack
+
+import concourse.mybir as mybir
+from concourse.masks import make_identity
+
+B, D, M = 1024, 2048, 1024
+FLOPS = 2 * B * D * M + 2 * B * M * D
+
+F32 = mybir.dt.float32
+BF16 = mybir.dt.bfloat16
+I32 = mybir.dt.int32
+U32 = mybir.dt.uint32
+U8 = mybir.dt.uint8
+FP4X4 = mybir.dt.float4_e2m1fn_x4
+FP8X4 = mybir.dt.float8_e4m3fn_x4
+ALU = mybir.AluOpType
+
+P = 128
+N = 512
+TILES = B // P
+G1 = D // 512
+G2 = M // 512
+QUARTERS = D // N
+BANKS = 8
+PINV_ROW = 4
+
+
+def tile_null_space_restoration_s4_kernel(
+    tc, x_words, x_scales, a_words, a_scales, pinv_words, pinv_scales, x0, y, mask, out
+):
+    nc = tc.nc
+    with ExitStack() as ctx:
+        keep = ctx.enter_context(tc.tile_pool(name="keep", bufs=1))
+        ring = ctx.enter_context(tc.tile_pool(name="ring", bufs=4))
+        psum = ctx.enter_context(tc.psum_pool(name="psum", bufs=1))
+        ctx.enter_context(tc.manual_schedule())
+
+        x_plane = keep.tile([P, G1, B], U8, name="x_plane", align_bytes=64)
+        a_plane = keep.tile([P, G1, M], U8, name="a_plane", align_bytes=64)
+        pinv_plane = keep.tile([P, G2, D], U8, name="pinv_plane", align_bytes=64)
+        for plane in (a_plane, x_plane, pinv_plane):
+            nc.vector.memset(plane[:].bitcast(I32), 0)
+        ident = keep.tile([P, P], F32, name="ident")
+        make_identity(nc, ident[:])
+
+        def load_scales(plane, scales, first_row):
+            for r in range(4):
+                nc.sync.dma_start(
+                    out=plane[first_row + r : P : 32, :, :].bitcast(I32),
+                    in_=scales.bitcast(I32)[:, r:16:4, :].rearrange("g q w -> q g w"),
+                )
+
+        a_sb, x_sb, pinv_sb, y_sb, mask_sb, x0_sb = {}, {}, {}, {}, {}, {}
+
+        def load_a(g):
+            a_sb[g] = keep.tile([P, 2 * M], U8, name="a%d" % g, align_bytes=64)
+            nc.sync.dma_start(out=a_sb[g][:].bitcast(I32), in_=a_words.bitcast(I32)[g])
+
+        def load_x(first, last):
+            t = keep.tile([P, G1, 2 * P * (last - first)], U8, name="x%d" % first, align_bytes=64)
+            src = x_words.bitcast(I32)[:, :, 64 * first : 64 * last].rearrange("g p w -> p g w")
+            nc.sync.dma_start(out=t[:].bitcast(I32), in_=src)
+            for i in range(first, last):
+                x_sb[i] = (t, i - first)
+
+        def load_pinv(q):
+            pinv_sb[q] = keep.tile([P, G2, N], U32, name="pinv%d" % q, align_bytes=64)
+            src = pinv_words.rearrange("g p n t -> p g (n t)")[:, :, 4 * N * q : 4 * N * (q + 1)]
+            nc.sync.dma_start(out=pinv_sb[q][:].bitcast(I32), in_=src.bitcast(I32))
+
+        def load_ym(i):
+            y_sb[i] = keep.tile([P, M], BF16, name="y%d" % i)
+            mask_sb[i] = keep.tile([P, M], BF16, name="mask%d" % i)
+            nc.sync.dma_start(out=y_sb[i][:], in_=y[P * i : P * (i + 1), :])
+            nc.sync.dma_start(out=mask_sb[i][:], in_=mask[P * i : P * (i + 1), :])
+
+        def load_x0(i):
+            x0_sb[i] = keep.tile([P, D], BF16, name="x0_%d" % i)
+            nc.sync.dma_start(out=x0_sb[i][:], in_=x0[P * i : P * (i + 1), :])
+
+        load_a(0)
+        load_x(0, 2)
+        load_scales(a_plane, a_scales, 0)
+        load_scales(x_plane, x_scales, 0)
+        for g in range(1, G1):
+            load_a(g)
+        load_ym(0)
+        load_ym(1)
+        load_x(2, 4)
+        load_ym(2)
+        load_scales(pinv_plane, pinv_scales, PINV_ROW)
+        load_ym(3)
+        load_x(4, TILES)
+        load_pinv(0)
+        load_pinv(1)
+        load_x0(0)
+        load_pinv(2)
+        load_pinv(3)
+        load_ym(4)
+        load_ym(5)
+        load_x0(1)
+        load_ym(6)
+        load_x0(2)
+        load_ym(7)
+        for i in range(3, TILES):
+            load_x0(i)
+
+        banks_used = []
+
+        def next_bank(shape):
+            name = "bank%d" % (len(banks_used) % BANKS)
+            banks_used.append(name)
+            return psum.tile(shape, F32, name=name, tag=name)
+
+        y_sorted, mask_sorted, r_sb, grouped, codes, r_plane = {}, {}, {}, {}, {}, {}
+
+        def sort_pairs(i):
+            y_sorted[i] = ring.tile([P, M], BF16, name="y_sorted")
+            mask_sorted[i] = ring.tile([P, M], BF16, name="mask_sorted")
+            for dst, src in ((y_sorted[i], y_sb[i]), (mask_sorted[i], mask_sb[i])):
+                nc.scalar.copy(
+                    out=dst[:].bitcast(F32).rearrange("p (g u j) -> p g u j", g=G2, u=2),
+                    in_=src[:].bitcast(F32).rearrange("p (g j u) -> p g u j", g=G2, u=2),
+                )
+
+        def measure_pass(acc, i, h, g):
+            t, j = x_sb[i]
+            nc.tensor.matmul_mx(
+                out=acc[:],
+                lhsT=t[:, g, 2 * P * j : 2 * P * (j + 1)].bitcast(FP4X4),
+                lhsT_scale=x_plane[:, g, P * i : P * (i + 1)],
+                rhs=a_sb[g][:, 2 * N * h : 2 * N * (h + 1)].bitcast(FP4X4),
+                rhs_scale=a_plane[:, g, N * h : N * (h + 1)],
+                start=(g == 0),
+                stop=(g == G1 - 1),
+            )
+
+        def residual(acc, i, h, engine):
+            cols = slice(N * h, N * (h + 1))
+            if h == 0:
+                r_sb[i] = ring.tile([P, M], BF16, name="r")
+            diff = ring.tile([P, N], F32, name="diff")
+            nc.vector.tensor_tensor(
+                out=diff[:].rearrange("p (u j e) -> p u j e", u=2, e=2),
+                in0=y_sorted[i][:, cols].rearrange("p (u j e) -> p u j e", u=2, e=2),
+                in1=acc[:].rearrange("p (j u e) -> p u j e", u=2, e=2),
+                op=ALU.subtract,
+            )
+            engine.tensor_tensor(out=r_sb[i][:, cols], in0=diff[:], in1=mask_sorted[i][:, cols], op=ALU.mult)
+
+        def measure(i):
+            sort_pairs(i)
+            for h in range(G2):
+                acc = next_bank([P, N])
+                for g in range(G1):
+                    measure_pass(acc, i, h, g)
+                residual(acc, i, h, nc.gpsimd)
+
+        def turn(i):
+            bank = next_bank([P, 2 * G2, P])
+            words = r_sb[i][:].bitcast(F32)
+            for s in range(2 * G2):
+                nc.tensor.transpose(bank[:, s, :], words[:, P * s : P * (s + 1)], ident[:])
+            grouped[i] = ring.tile([P, M], BF16, name="grouped", align_bytes=64)
+            nc.scalar.copy(
+                out=grouped[i][:].bitcast(F32).rearrange("p (g b u) -> p g b u", g=G2, u=2),
+                in_=bank[:].rearrange("p (g u) b -> p g b u", u=2),
+            )
+
+        def quantize(i):
+            codes[i] = ring.tile([P, G2 * P], U32, name="codes", align_bytes=64)
+            r_plane[i] = ring.tile([P, G2 * P], U8, name="r_plane", align_bytes=64)
+            nc.vector.quantize_mx(out=codes[i][:].bitcast(FP8X4), scales=r_plane[i][:], in_=grouped[i][:])
+
+        def restore(i, after_first, after_last):
+            width = N if i == TILES - 1 else 2 * N
+            for q in range(QUARTERS):
+                acc = next_bank([P, N])
+                for g in range(G2):
+                    nc.tensor.matmul_mx(
+                        out=acc[:],
+                        lhsT=codes[i][:, P * g : P * (g + 1)].bitcast(FP8X4),
+                        lhsT_scale=r_plane[i][:, P * g : P * (g + 1)],
+                        rhs=pinv_sb[q][:, g, :].bitcast(FP8X4),
+                        rhs_scale=pinv_plane[PINV_ROW:P, g, N * q : N * (q + 1)],
+                        start=(g == 0),
+                        stop=(g == G2 - 1),
+                    )
+                start = N * q % width
+                if start == 0:
+                    piece = keep.tile([P, width], F32, name="out%d_%d" % (i, q))
+                nc.vector.tensor_tensor(
+                    out=piece[:, start : start + N], in0=acc[:], in1=x0_sb[i][:, N * q : N * (q + 1)], op=ALU.add
+                )
+                if start + N == width:
+                    first = N * (q + 1) - width
+                    nc.sync.dma_start(out=out[P * i : P * (i + 1), first : first + width], in_=piece[:])
+                if q == 0 and after_first is not None:
+                    quantize(after_first)
+            if after_last is not None:
+                quantize(after_last)
+
+        sort_pairs(0)
+        sort_pairs(1)
+        head = [(i, h, next_bank([P, N])) for i in range(2) for h in range(G2)]
+        for g in range(G1):
+            for i, h, acc in head:
+                measure_pass(acc, i, h, g)
+        for i, h, acc in head:
+            residual(acc, i, h, nc.vector)
+        measure(2)
+        measure(3)
+        for j in range(TILES // 2):
+            turn(2 * j)
+            turn(2 * j + 1)
+            if j == 0:
+                quantize(0)
+                quantize(1)
+            else:
+                restore(2 * j - 1, 2 * j, 2 * j + 1)
+            if 2 * j + 4 < TILES:
+                measure(2 * j + 4)
+            restore(2 * j, None, None)
+            if 2 * j + 5 < TILES:
+                measure(2 * j + 5)
+        restore(TILES - 1, None, None)

@@ -35,75 +35,86 @@ def tile_null_space_restoration_s4_kernel(
         psum = ctx.enter_context(tc.psum_pool(name="psum", bufs=1))
         ctx.enter_context(tc.manual_schedule())
 
-        x_plane = keep.tile([P, G1, B], U8, name="x_plane", align_bytes=64)
-        a_plane = keep.tile([P, G1, M], U8, name="a_plane", align_bytes=64)
-        pinv_plane = keep.tile([P, G2, D], U8, name="pinv_plane", align_bytes=64)
-        for plane in (a_plane, x_plane, pinv_plane):
-            nc.vector.memset(plane[:].bitcast(I32), 0)
-        ident = keep.tile([P, P], F32, name="ident")
-        make_identity(nc, ident[:])
+        def scale_plane(name, scales, first, last, clear):
+            groups = scales.shape[0]
+            plane = keep.tile([P, groups, last - first], U8, name=name, align_bytes=64)
+            clear.memset(plane[:].bitcast(I32), 0)
+            return plane, scales.bitcast(I32)[:, :, first // 4 : last // 4]
 
-        def load_scales(plane, scales, first_row):
-            for r in range(4):
-                nc.sync.dma_start(
-                    out=plane[first_row + r : P : 32, :, :].bitcast(I32),
-                    in_=scales.bitcast(I32)[:, r:16:4, :].rearrange("g q w -> q g w"),
-                )
+        def load_scales(queue, plane, rows, r, first_row):
+            queue.dma_start(
+                out=plane[first_row + r : P : 32, :, :].bitcast(I32),
+                in_=rows[:, r:16:4, :].rearrange("g q w -> q g w"),
+            )
+
+        def load_quadrant_scales(queue, plane, rows, q):
+            queue.dma_start(
+                out=plane[32 * q : 32 * q + 4, :, :].bitcast(I32),
+                in_=rows[:, 4 * q : 4 * q + 4, :].rearrange("g r w -> r g w"),
+            )
 
         a_sb, x_sb, pinv_sb, y_sb, mask_sb, x0_sb = {}, {}, {}, {}, {}, {}
 
-        def load_a(g):
-            a_sb[g] = keep.tile([P, 2 * M], U8, name="a%d" % g, align_bytes=64)
-            nc.sync.dma_start(out=a_sb[g][:].bitcast(I32), in_=a_words.bitcast(I32)[g])
+        def load_a(first, last):
+            t = keep.tile([P, last - first, 2 * M], U8, name="a%d" % first, align_bytes=64)
+            nc.sync.dma_start(out=t[:].bitcast(I32), in_=a_words.bitcast(I32)[first:last].rearrange("g p w -> p g w"))
+            for g in range(first, last):
+                a_sb[g] = t[:, g - first, :]
 
-        def load_x(first, last):
+        def load_x(first, last, plane):
             t = keep.tile([P, G1, 2 * P * (last - first)], U8, name="x%d" % first, align_bytes=64)
             src = x_words.bitcast(I32)[:, :, 64 * first : 64 * last].rearrange("g p w -> p g w")
             nc.sync.dma_start(out=t[:].bitcast(I32), in_=src)
             for i in range(first, last):
-                x_sb[i] = (t, i - first)
+                x_sb[i] = (t, plane, i - first)
 
-        def load_pinv(q):
-            pinv_sb[q] = keep.tile([P, G2, N], U32, name="pinv%d" % q, align_bytes=64)
-            src = pinv_words.rearrange("g p n t -> p g (n t)")[:, :, 4 * N * q : 4 * N * (q + 1)]
-            nc.sync.dma_start(out=pinv_sb[q][:].bitcast(I32), in_=src.bitcast(I32))
+        def load_pinv(half):
+            t = keep.tile([P, G2, 2 * N], U32, name="pinv%d" % half, align_bytes=64)
+            src = pinv_words.rearrange("g p n t -> p g (n t)")[:, :, 8 * N * half : 8 * N * (half + 1)]
+            nc.sync.dma_start(out=t[:].bitcast(I32), in_=src.bitcast(I32))
+            pinv_sb[half] = t
 
-        def load_ym(i):
-            y_sb[i] = keep.tile([P, M], BF16, name="y%d" % i)
-            mask_sb[i] = keep.tile([P, M], BF16, name="mask%d" % i)
-            nc.sync.dma_start(out=y_sb[i][:], in_=y[P * i : P * (i + 1), :])
-            nc.sync.dma_start(out=mask_sb[i][:], in_=mask[P * i : P * (i + 1), :])
+        def load_rows(held, name, src, first, last):
+            t = keep.tile([P, last - first, src.shape[1]], BF16, name="%s%d" % (name, first))
+            nc.sync.dma_start(out=t[:], in_=src[P * first : P * last, :].rearrange("(i p) c -> p i c", p=P))
+            for i in range(first, last):
+                held[i] = t[:, i - first, :]
 
-        def load_x0(i):
-            x0_sb[i] = keep.tile([P, D], BF16, name="x0_%d" % i)
-            nc.sync.dma_start(out=x0_sb[i][:], in_=x0[P * i : P * (i + 1), :])
+        a_plane, a_rows = scale_plane("a_plane", a_scales, 0, M, nc.vector)
+        x_head_plane, x_head_rows = scale_plane("x_head_plane", x_scales, 0, 2 * P, nc.gpsimd)
+        for q in (2, 3):
+            load_quadrant_scales(nc.gpsimd, x_head_plane, x_head_rows, q)
+        x_rest_plane, x_rest_rows = scale_plane("x_rest_plane", x_scales, 2 * P, B, nc.vector)
+        pinv_plane, pinv_rows = scale_plane("pinv_plane", pinv_scales, 0, D, nc.gpsimd)
+        for r in range(4):
+            load_scales(nc.gpsimd, pinv_plane, pinv_rows, r, PINV_ROW)
+        ident = keep.tile([P, P], F32, name="ident")
+        make_identity(nc, ident[:])
 
-        load_a(0)
-        load_x(0, 2)
-        load_scales(a_plane, a_scales, 0)
-        load_scales(x_plane, x_scales, 0)
-        for g in range(1, G1):
-            load_a(g)
-        load_ym(0)
-        load_ym(1)
-        load_x(2, 4)
-        load_ym(2)
-        load_scales(pinv_plane, pinv_scales, PINV_ROW)
-        load_ym(3)
-        load_x(4, TILES)
+        load_a(0, 1)
+        load_x(0, 2, x_head_plane)
+        for q in (0, 1):
+            load_quadrant_scales(nc.sync, x_head_plane, x_head_rows, q)
+        for r in range(4):
+            load_scales(nc.sync, a_plane, a_rows, r, 0)
+        load_a(1, G1)
+        load_rows(y_sb, "y", y, 0, 2)
+        for r in range(4):
+            load_scales(nc.sync, x_rest_plane, x_rest_rows, r, 0)
+        load_rows(mask_sb, "mask", mask, 0, 2)
+        load_x(2, TILES, x_rest_plane)
+        load_rows(y_sb, "y", y, 2, 4)
+        load_rows(mask_sb, "mask", mask, 2, 4)
         load_pinv(0)
+        load_rows(y_sb, "y", y, 4, 6)
         load_pinv(1)
-        load_x0(0)
-        load_pinv(2)
-        load_pinv(3)
-        load_ym(4)
-        load_ym(5)
-        load_x0(1)
-        load_ym(6)
-        load_x0(2)
-        load_ym(7)
-        for i in range(3, TILES):
-            load_x0(i)
+        load_rows(x0_sb, "x0", x0, 0, 1)
+        load_rows(mask_sb, "mask", mask, 4, 6)
+        load_rows(x0_sb, "x0", x0, 1, 2)
+        load_rows(y_sb, "y", y, 6, 8)
+        load_rows(mask_sb, "mask", mask, 6, 8)
+        for i in range(2, TILES, 2):
+            load_rows(x0_sb, "x0", x0, i, i + 2)
 
         banks_used = []
 
@@ -120,15 +131,15 @@ def tile_null_space_restoration_s4_kernel(
             for dst, src in ((y_sorted[i], y_sb[i]), (mask_sorted[i], mask_sb[i])):
                 nc.scalar.copy(
                     out=dst[:].bitcast(F32).rearrange("p (g u j) -> p g u j", g=G2, u=2),
-                    in_=src[:].bitcast(F32).rearrange("p (g j u) -> p g u j", g=G2, u=2),
+                    in_=src.bitcast(F32).rearrange("p (g j u) -> p g u j", g=G2, u=2),
                 )
 
         def measure_pass(acc, i, h, g):
-            t, j = x_sb[i]
+            t, plane, j = x_sb[i]
             nc.tensor.matmul_mx(
                 out=acc[:],
                 lhsT=t[:, g, 2 * P * j : 2 * P * (j + 1)].bitcast(FP4X4),
-                lhsT_scale=x_plane[:, g, P * i : P * (i + 1)],
+                lhsT_scale=plane[:, g, P * j : P * (j + 1)],
                 rhs=a_sb[g][:, 2 * N * h : 2 * N * (h + 1)].bitcast(FP4X4),
                 rhs_scale=a_plane[:, g, N * h : N * (h + 1)],
                 start=(g == 0),
@@ -173,7 +184,7 @@ def tile_null_space_restoration_s4_kernel(
             nc.vector.quantize_mx(out=codes[i][:].bitcast(FP8X4), scales=r_plane[i][:], in_=grouped[i][:])
 
         def restore(i, after_first, after_last):
-            width = N if i == TILES - 1 else 2 * N
+            width = {TILES - 1: N, TILES - 2: 2 * N}.get(i, D)
             for q in range(QUARTERS):
                 acc = next_bank([P, N])
                 for g in range(G2):
@@ -181,7 +192,7 @@ def tile_null_space_restoration_s4_kernel(
                         out=acc[:],
                         lhsT=codes[i][:, P * g : P * (g + 1)].bitcast(FP8X4),
                         lhsT_scale=r_plane[i][:, P * g : P * (g + 1)],
-                        rhs=pinv_sb[q][:, g, :].bitcast(FP8X4),
+                        rhs=pinv_sb[q // 2][:, g, N * (q % 2) : N * (q % 2 + 1)].bitcast(FP8X4),
                         rhs_scale=pinv_plane[PINV_ROW:P, g, N * q : N * (q + 1)],
                         start=(g == 0),
                         stop=(g == G2 - 1),

@@ -80,11 +80,13 @@ def tile_null_space_restoration_s4_kernel(
             for i in range(first, last):
                 held[i] = t[:, i - first, :]
 
+        x_head_plane, x_head_rows = scale_plane("x_head_plane", x_scales, 0, 2 * P, nc.vector)
         a_plane, a_rows = scale_plane("a_plane", a_scales, 0, M, nc.vector)
-        x_head_plane, x_head_rows = scale_plane("x_head_plane", x_scales, 0, 2 * P, nc.gpsimd)
         for q in (2, 3):
             load_quadrant_scales(nc.gpsimd, x_head_plane, x_head_rows, q)
         x_rest_plane, x_rest_rows = scale_plane("x_rest_plane", x_scales, 2 * P, B, nc.vector)
+        for r in range(4):
+            load_scales(nc.gpsimd, x_rest_plane, x_rest_rows, r, 0)
         pinv_plane, pinv_rows = scale_plane("pinv_plane", pinv_scales, 0, D, nc.gpsimd)
         for r in range(4):
             load_scales(nc.gpsimd, pinv_plane, pinv_rows, r, PINV_ROW)
@@ -99,8 +101,6 @@ def tile_null_space_restoration_s4_kernel(
             load_scales(nc.sync, a_plane, a_rows, r, 0)
         load_a(1, G1)
         load_rows(y_sb, "y", y, 0, 2)
-        for r in range(4):
-            load_scales(nc.sync, x_rest_plane, x_rest_rows, r, 0)
         load_rows(mask_sb, "mask", mask, 0, 2)
         load_x(2, TILES, x_rest_plane)
         load_rows(y_sb, "y", y, 2, 4)
@@ -146,26 +146,39 @@ def tile_null_space_restoration_s4_kernel(
                 stop=(g == G1 - 1),
             )
 
-        def residual(acc, i, h, engine):
-            cols = slice(N * h, N * (h + 1))
-            if h == 0:
-                r_sb[i] = ring.tile([P, M], BF16, name="r")
+        def subtract(acc, i, h):
             diff = ring.tile([P, N], F32, name="diff")
             nc.vector.tensor_tensor(
                 out=diff[:].rearrange("p (u j e) -> p u j e", u=2, e=2),
-                in0=y_sorted[i][:, cols].rearrange("p (u j e) -> p u j e", u=2, e=2),
+                in0=y_sorted[i][:, N * h : N * (h + 1)].rearrange("p (u j e) -> p u j e", u=2, e=2),
                 in1=acc[:].rearrange("p (j u e) -> p u j e", u=2, e=2),
                 op=ALU.subtract,
             )
+            return diff
+
+        def apply_mask(engine, diff, i, h):
+            cols = slice(N * h, N * (h + 1))
+            if h == 0:
+                r_sb[i] = ring.tile([P, M], BF16, name="r")
             engine.tensor_tensor(out=r_sb[i][:, cols], in0=diff[:], in1=mask_sorted[i][:, cols], op=ALU.mult)
+
+        def residual_on_vector(i, accs):
+            diffs = [subtract(accs[h], i, h) for h in range(G2)]
+            for h in range(G2):
+                apply_mask(nc.vector, diffs[h], i, h)
 
         def measure(i):
             sort_pairs(i)
+            accs = [next_bank([P, N]) for h in range(G2)]
             for h in range(G2):
-                acc = next_bank([P, N])
                 for g in range(G1):
-                    measure_pass(acc, i, h, g)
-                residual(acc, i, h, nc.gpsimd)
+                    measure_pass(accs[h], i, h, g)
+            return accs
+
+        def measure_and_mask(i):
+            accs = measure(i)
+            for h in range(G2):
+                apply_mask(nc.gpsimd, subtract(accs[h], i, h), i, h)
 
         def turn(i):
             bank = next_bank([P, 2 * G2, P])
@@ -184,7 +197,7 @@ def tile_null_space_restoration_s4_kernel(
             nc.vector.quantize_mx(out=codes[i][:].bitcast(FP8X4), scales=r_plane[i][:], in_=grouped[i][:])
 
         def restore(i, after_first, after_last):
-            width = {TILES - 1: N, TILES - 2: 2 * N}.get(i, D)
+            width = N if i == TILES - 1 else (D if i < 3 else 2 * N)
             for q in range(QUARTERS):
                 acc = next_bank([P, N])
                 for g in range(G2):
@@ -201,7 +214,7 @@ def tile_null_space_restoration_s4_kernel(
                 if start == 0:
                     piece = keep.tile([P, width], F32, name="out%d_%d" % (i, q))
                 nc.vector.tensor_tensor(
-                    out=piece[:, start : start + N], in0=acc[:], in1=x0_sb[i][:, N * q : N * (q + 1)], op=ALU.add
+                    out=piece[:, start : start + N], in0=x0_sb[i][:, N * q : N * (q + 1)], in1=acc[:], op=ALU.add
                 )
                 if start + N == width:
                     first = N * (q + 1) - width
@@ -213,25 +226,27 @@ def tile_null_space_restoration_s4_kernel(
 
         sort_pairs(0)
         sort_pairs(1)
-        head = [(i, h, next_bank([P, N])) for i in range(2) for h in range(G2)]
+        head = [[next_bank([P, N]) for h in range(G2)] for i in range(2)]
         for g in range(G1):
-            for i, h, acc in head:
-                measure_pass(acc, i, h, g)
-        for i, h, acc in head:
-            residual(acc, i, h, nc.vector)
-        measure(2)
-        measure(3)
+            for i in range(2):
+                for h in range(G2):
+                    measure_pass(head[i][h], i, h, g)
+        for i in range(2):
+            residual_on_vector(i, head[i])
+        residual_on_vector(2, measure(2))
+        third = measure(3)
         for j in range(TILES // 2):
             turn(2 * j)
             turn(2 * j + 1)
             if j == 0:
                 quantize(0)
+                residual_on_vector(3, third)
                 quantize(1)
             else:
                 restore(2 * j - 1, 2 * j, 2 * j + 1)
             if 2 * j + 4 < TILES:
-                measure(2 * j + 4)
+                measure_and_mask(2 * j + 4)
             restore(2 * j, None, None)
             if 2 * j + 5 < TILES:
-                measure(2 * j + 5)
+                measure_and_mask(2 * j + 5)
         restore(TILES - 1, None, None)

from contextlib import ExitStack

import concourse.mybir as mybir
from concourse.masks import make_identity

B, D, M = 1024, 2048, 1024
FLOPS = 2 * B * D * M + 2 * B * M * D

F32 = mybir.dt.float32
BF16 = mybir.dt.bfloat16
I32 = mybir.dt.int32
U32 = mybir.dt.uint32
U8 = mybir.dt.uint8
FP4X4 = mybir.dt.float4_e2m1fn_x4
FP8X4 = mybir.dt.float8_e4m3fn_x4
ALU = mybir.AluOpType

P = 128
N = 512
TILES = B // P
G1 = D // 512
G2 = M // 512
QUARTERS = D // N
BANKS = 8
PINV_ROW = 4


def tile_null_space_restoration_s4_kernel(
    tc, x_words, x_scales, a_words, a_scales, pinv_words, pinv_scales, x0, y, mask, out
):
    nc = tc.nc
    with ExitStack() as ctx:
        keep = ctx.enter_context(tc.tile_pool(name="keep", bufs=1))
        ring = ctx.enter_context(tc.tile_pool(name="ring", bufs=4))
        psum = ctx.enter_context(tc.psum_pool(name="psum", bufs=1))
        ctx.enter_context(tc.manual_schedule())

        def scale_plane(name, scales, first, last, clear):
            groups = scales.shape[0]
            plane = keep.tile([P, groups, last - first], U8, name=name, align_bytes=64)
            clear.memset(plane[:].bitcast(I32), 0)
            return plane, scales.bitcast(I32)[:, :, first // 4 : last // 4]

        def load_scales(queue, plane, rows, r, first_row):
            queue.dma_start(
                out=plane[first_row + r : P : 32, :, :].bitcast(I32),
                in_=rows[:, r:16:4, :].rearrange("g q w -> q g w"),
            )

        def load_quadrant_scales(queue, plane, rows, q):
            queue.dma_start(
                out=plane[32 * q : 32 * q + 4, :, :].bitcast(I32),
                in_=rows[:, 4 * q : 4 * q + 4, :].rearrange("g r w -> r g w"),
            )

        a_sb, x_sb, pinv_sb, y_sb, mask_sb, x0_sb = {}, {}, {}, {}, {}, {}

        def load_a(first, last):
            t = keep.tile([P, last - first, 2 * M], U8, name="a%d" % first, align_bytes=64)
            nc.sync.dma_start(out=t[:].bitcast(I32), in_=a_words.bitcast(I32)[first:last].rearrange("g p w -> p g w"))
            for g in range(first, last):
                a_sb[g] = t[:, g - first, :]

        def load_x(first, last, plane):
            t = keep.tile([P, G1, 2 * P * (last - first)], U8, name="x%d" % first, align_bytes=64)
            src = x_words.bitcast(I32)[:, :, 64 * first : 64 * last].rearrange("g p w -> p g w")
            nc.sync.dma_start(out=t[:].bitcast(I32), in_=src)
            for i in range(first, last):
                x_sb[i] = (t, plane, i - first)

        def load_pinv(half):
            t = keep.tile([P, G2, 2 * N], U32, name="pinv%d" % half, align_bytes=64)
            src = pinv_words.rearrange("g p n t -> p g (n t)")[:, :, 8 * N * half : 8 * N * (half + 1)]
            nc.sync.dma_start(out=t[:].bitcast(I32), in_=src.bitcast(I32))
            pinv_sb[half] = t

        def load_rows(held, name, src, first, last):
            t = keep.tile([P, last - first, src.shape[1]], BF16, name="%s%d" % (name, first))
            nc.sync.dma_start(out=t[:], in_=src[P * first : P * last, :].rearrange("(i p) c -> p i c", p=P))
            for i in range(first, last):
                held[i] = t[:, i - first, :]

        x_head_plane, x_head_rows = scale_plane("x_head_plane", x_scales, 0, 2 * P, nc.vector)
        a_plane, a_rows = scale_plane("a_plane", a_scales, 0, M, nc.vector)
        for q in (2, 3):
            load_quadrant_scales(nc.gpsimd, x_head_plane, x_head_rows, q)
        x_rest_plane, x_rest_rows = scale_plane("x_rest_plane", x_scales, 2 * P, B, nc.vector)
        for r in range(4):
            load_scales(nc.gpsimd, x_rest_plane, x_rest_rows, r, 0)
        pinv_plane, pinv_rows = scale_plane("pinv_plane", pinv_scales, 0, D, nc.gpsimd)
        for r in range(4):
            load_scales(nc.gpsimd, pinv_plane, pinv_rows, r, PINV_ROW)
        ident = keep.tile([P, P], F32, name="ident")
        make_identity(nc, ident[:])

        load_a(0, 1)
        load_x(0, 2, x_head_plane)
        for q in (0, 1):
            load_quadrant_scales(nc.sync, x_head_plane, x_head_rows, q)
        for r in range(4):
            load_scales(nc.sync, a_plane, a_rows, r, 0)
        load_a(1, G1)
        load_rows(y_sb, "y", y, 0, 2)
        load_rows(mask_sb, "mask", mask, 0, 2)
        load_x(2, TILES, x_rest_plane)
        load_rows(y_sb, "y", y, 2, 4)
        load_rows(mask_sb, "mask", mask, 2, 4)
        load_pinv(0)
        load_rows(y_sb, "y", y, 4, 6)
        load_pinv(1)
        load_rows(x0_sb, "x0", x0, 0, 1)
        load_rows(mask_sb, "mask", mask, 4, 6)
        load_rows(x0_sb, "x0", x0, 1, 2)
        load_rows(y_sb, "y", y, 6, 8)
        load_rows(mask_sb, "mask", mask, 6, 8)
        for i in range(2, TILES, 2):
            load_rows(x0_sb, "x0", x0, i, i + 2)

        banks_used = []

        def next_bank(shape):
            name = "bank%d" % (len(banks_used) % BANKS)
            banks_used.append(name)
            return psum.tile(shape, F32, name=name, tag=name)

        y_sorted, mask_sorted, r_sb, grouped, codes, r_plane = {}, {}, {}, {}, {}, {}

        def sort_pairs(i):
            y_sorted[i] = ring.tile([P, M], BF16, name="y_sorted")
            mask_sorted[i] = ring.tile([P, M], BF16, name="mask_sorted")
            for dst, src in ((y_sorted[i], y_sb[i]), (mask_sorted[i], mask_sb[i])):
                nc.scalar.copy(
                    out=dst[:].bitcast(F32).rearrange("p (g u j) -> p g u j", g=G2, u=2),
                    in_=src.bitcast(F32).rearrange("p (g j u) -> p g u j", g=G2, u=2),
                )

        def measure_pass(acc, i, h, g):
            t, plane, j = x_sb[i]
            nc.tensor.matmul_mx(
                out=acc[:],
                lhsT=t[:, g, 2 * P * j : 2 * P * (j + 1)].bitcast(FP4X4),
                lhsT_scale=plane[:, g, P * j : P * (j + 1)],
                rhs=a_sb[g][:, 2 * N * h : 2 * N * (h + 1)].bitcast(FP4X4),
                rhs_scale=a_plane[:, g, N * h : N * (h + 1)],
                start=(g == 0),
                stop=(g == G1 - 1),
            )

        def subtract(acc, i, h):
            diff = ring.tile([P, N], F32, name="diff")
            nc.vector.tensor_tensor(
                out=diff[:].rearrange("p (u j e) -> p u j e", u=2, e=2),
                in0=y_sorted[i][:, N * h : N * (h + 1)].rearrange("p (u j e) -> p u j e", u=2, e=2),
                in1=acc[:].rearrange("p (j u e) -> p u j e", u=2, e=2),
                op=ALU.subtract,
            )
            return diff

        def apply_mask(engine, diff, i, h):
            cols = slice(N * h, N * (h + 1))
            if h == 0:
                r_sb[i] = ring.tile([P, M], BF16, name="r")
            engine.tensor_tensor(out=r_sb[i][:, cols], in0=diff[:], in1=mask_sorted[i][:, cols], op=ALU.mult)

        def residual_on_vector(i, accs):
            diffs = [subtract(accs[h], i, h) for h in range(G2)]
            for h in range(G2):
                apply_mask(nc.vector, diffs[h], i, h)

        def measure(i):
            sort_pairs(i)
            accs = [next_bank([P, N]) for h in range(G2)]
            for h in range(G2):
                for g in range(G1):
                    measure_pass(accs[h], i, h, g)
            return accs

        def measure_and_mask(i):
            accs = measure(i)
            for h in range(G2):
                apply_mask(nc.gpsimd, subtract(accs[h], i, h), i, h)

        def turn(i):
            bank = next_bank([P, 2 * G2, P])
            words = r_sb[i][:].bitcast(F32)
            for s in range(2 * G2):
                nc.tensor.transpose(bank[:, s, :], words[:, P * s : P * (s + 1)], ident[:])
            grouped[i] = ring.tile([P, M], BF16, name="grouped", align_bytes=64)
            nc.scalar.copy(
                out=grouped[i][:].bitcast(F32).rearrange("p (g b u) -> p g b u", g=G2, u=2),
                in_=bank[:].rearrange("p (g u) b -> p g b u", u=2),
            )

        def quantize(i):
            codes[i] = ring.tile([P, G2 * P], U32, name="codes", align_bytes=64)
            r_plane[i] = ring.tile([P, G2 * P], U8, name="r_plane", align_bytes=64)
            nc.vector.quantize_mx(out=codes[i][:].bitcast(FP8X4), scales=r_plane[i][:], in_=grouped[i][:])

        def restore(i, after_first, after_last):
            width = N if i == TILES - 1 else (D if i < 3 else 2 * N)
            for q in range(QUARTERS):
                acc = next_bank([P, N])
                for g in range(G2):
                    nc.tensor.matmul_mx(
                        out=acc[:],
                        lhsT=codes[i][:, P * g : P * (g + 1)].bitcast(FP8X4),
                        lhsT_scale=r_plane[i][:, P * g : P * (g + 1)],
                        rhs=pinv_sb[q // 2][:, g, N * (q % 2) : N * (q % 2 + 1)].bitcast(FP8X4),
                        rhs_scale=pinv_plane[PINV_ROW:P, g, N * q : N * (q + 1)],
                        start=(g == 0),
                        stop=(g == G2 - 1),
                    )
                start = N * q % width
                if start == 0:
                    piece = keep.tile([P, width], F32, name="out%d_%d" % (i, q))
                nc.vector.tensor_tensor(
                    out=piece[:, start : start + N], in0=x0_sb[i][:, N * q : N * (q + 1)], in1=acc[:], op=ALU.add
                )
                if start + N == width:
                    first = N * (q + 1) - width
                    nc.sync.dma_start(out=out[P * i : P * (i + 1), first : first + width], in_=piece[:])
                if q == 0 and after_first is not None:
                    quantize(after_first)
            if after_last is not None:
                quantize(after_last)

        sort_pairs(0)
        sort_pairs(1)
        head = [[next_bank([P, N]) for h in range(G2)] for i in range(2)]
        for g in range(G1):
            for i in range(2):
                for h in range(G2):
                    measure_pass(head[i][h], i, h, g)
        for i in range(2):
            residual_on_vector(i, head[i])
        residual_on_vector(2, measure(2))
        third = measure(3)
        for j in range(TILES // 2):
            turn(2 * j)
            turn(2 * j + 1)
            if j == 0:
                quantize(0)
                residual_on_vector(3, third)
                quantize(1)
            else:
                restore(2 * j - 1, 2 * j, 2 * j + 1)
            if 2 * j + 4 < TILES:
                measure_and_mask(2 * j + 4)
            restore(2 * j, None, None)
            if 2 * j + 5 < TILES:
                measure_and_mask(2 * j + 5)
        restore(TILES - 1, None, None)
